import numpy as np, ml_dtypes
CORES = [4,20,36,44,92,100,108,116,3,19,35,43,91,99,107,115]
N = 16
TK = 512
WID = [256,128,448,192,64,512,320,64,64,512,320,512,128,64,256,256]
def setup_inputs(rng):
    return {"x": rng.standard_normal((N, 128, TK), dtype=np.float32).astype(ml_dtypes.bfloat16), "w1": (rng.standard_normal((N, 128, 128), dtype=np.float32) / 8).astype(ml_dtypes.bfloat16), "w2": (rng.standard_normal((N, 128, 128), dtype=np.float32) / 8).astype(ml_dtypes.bfloat16)}
def setup_inputs_big(rng):
    d = setup_inputs(rng)
    for k in ("x", "w1", "w2"): d[k] = (d[k].astype(np.float32) * 1024.0).astype(d[k].dtype)
    return d
def setup_inputs_small(rng):
    d = setup_inputs(rng)
    for k in ("x", "w1", "w2"): d[k] = (d[k].astype(np.float32) * (1 / 1024.0)).astype(d[k].dtype)
    return d
def setup_inputs_apart(rng):
    d = setup_inputs(rng)
    f = (10.0 ** rng.permutation(np.linspace(-1.5, 1.5, N))).astype(np.float32).reshape(N, 1, 1)
    for k in ("x", "w1", "w2"): d[k] = (d[k].astype(np.float32) * f).astype(d[k].dtype)
    return d
def whole(x, w1, w2):
    X, W1, W2 = x.astype(np.float64), w1.astype(np.float64), w2.astype(np.float64)
    y = np.zeros((N, 128, TK))
    for r in range(N):
        for j in range(N):
            y[r] += W2[j].T @ np.maximum(W1[j].T @ X[r], 0.0)
    return {"y": y.astype(ml_dtypes.bfloat16 if x.dtype != np.float64 else np.float64)}
def reference(x, w1, w2):
    o = whole(x, w1, w2)["y"].copy()
    for r in range(N):
        o[r][:, WID[r]:] = np.nan
    return {"y": o}

@@ -1,0 +1,197 @@
+from concourse.mybir import AluOpType
+
+H = 3
+LOOK = 1
+NSLOT = 8
+WW = 256
+RELAY_LAG = 5
+
+SCRATCH = {
+    "wbuf": ("sbuf", [128, NSLOT * WW], "bfloat16"),
+    "xbuf": ("sbuf", [128, 1024], "bfloat16"),
+    "zero": ("sbuf", [128, 512], "float32"),
+    "ysend": ("sbuf", [128, 512], "bfloat16"),
+    "yrecv": ("sbuf", [128, 512], "bfloat16"),
+    "yout": ("sbuf", [128, 512], "bfloat16"),
+    "yp0": ("psum", [128, 512], "float32"),
+    "yp1": ("psum", [128, 512], "float32"),
+}
+for _b in range(H):
+    SCRATCH["hs%d" % _b] = ("sbuf", [128, 512], "bfloat16")
+    SCRATCH["hp%d" % _b] = ("psum", [128, 512], "float32")
+
+SEMAPHORES = (["ldw", "ldx", "xa", "zr", "ys", "yr", "yo", "st", "sent"]
+              + ["wa%d" % s for s in range(NSLOT)]
+              + ["ma%d" % b for b in range(H)] + ["re%d" % b for b in range(H)] + ["mb%d" % b for b in range(H)])
+
+
+def _bits(m):
+    return bin(m).count("1")
+
+
+def _plan(T, topo):
+    cores = list(T.cores)
+    chips = sorted(set(topo.chip(c) for c in cores))
+    n = len(chips)
+    cidx = dict((ch, i) for i, ch in enumerate(chips))
+    site = dict(((topo.chip(c), topo.die(c)), c) for c in cores)
+    everyone = range(topo.CORES_PER_CHIP * topo.CHIPS)
+    sends, relay, eta = {}, {}, {}
+    for s in cores:
+        i, d = cidx[topo.chip(s)], topo.die(s)
+        tg = [site[(chips[(i + k) % n], d)] for k in range(1, n)]
+        direct = [t for t in tg if topo.may_write(s, t)]
+        cross = [t for t in tg if not topo.may_write(s, t)]
+        helpers = []
+        if cross:
+            helpers = [c for c in everyone
+                       if topo.chip(c) == topo.chip(s) and topo.die(c) == d and c not in cores
+                       and all(topo.may_write(c, t) for t in cross)]
+            helpers = helpers[:len(cross)]
+        for hi, hc in enumerate(helpers):
+            job = cross[hi::len(helpers)]
+            job = job[i % len(job):] + job[:i % len(job)]
+            relay[hc] = (i, job)
+            for q, t in enumerate(job):
+                eta[(t, i)] = hi + 1 + RELAY_LAG + q
+        for p, t in enumerate(direct):
+            eta[(t, i)] = len(helpers) + 2 + p
+        sends[s] = (helpers, direct)
+    order = {}
+    for t in cores:
+        me = cidx[topo.chip(t)]
+        rest = sorted((s for s in range(n) if s != me), key=lambda s: (eta[(t, s)], s))
+        order[t] = [me] + rest
+    return dict(cores=cores, chips=chips, cidx=cidx, sends=sends, relay=relay, order=order)
+
+
+def _narrow(T, topo, core):
+    m = -1
+    for c in T.cores:
+        if c != core:
+            m &= topo.mask(core, c)
+    return m
+
+
+def _put(g, T, topo, dst, out_ap, in_ap, rsem, mask):
+    rid, pid, _se = topo.addr(dst)
+    g.remote_dma(out_ap=out_ap, in_ap=in_ap, remote_sem=rsem, local_sem=T.sem.sent, pid=pid, routing_id=rid,
+                 dma_engine_mask=mask)
+    return _bits(mask)
+
+
+def rank_program(g, core, T, topo):
+    P = _plan(T, topo)
+    mask = _narrow(T, topo, core)
+    ne = _bits(mask)
+
+    if core in P["relay"]:
+        slot, job = P["relay"][core]
+        blk = T.wbuf[:, slot * WW:(slot + 1) * WW]
+        g.wait_ge(T.sem["wa%d" % slot], ne)
+        sent = 0
+        for t in job:
+            sent += _put(g, T, topo, t, blk, blk, T.sem["wa%d" % slot], mask)
+        g.wait_ge(T.sem.sent, sent)
+        return
+
+    rank = T.rank_of(core)
+    if rank is None:
+        return
+    wid = T.tables["WID"]
+    mates = [c for c in P["cores"] if topo.chip(c) == topo.chip(core)]
+    sib = [c for c in mates if c != core][0]
+    width = {0: wid[rank], 1: wid[T.rank_of(sib)]}
+    off, o = {}, 0
+    for c in mates:
+        off[c] = o
+        o += wid[T.rank_of(c)]
+    xcol = {0: off[core], 1: off[sib]}
+    me = P["cidx"][topo.chip(core)]
+    te, ve, sy, sc = g.tensor, g.vector, g.sync, g.scalar
+    myblk = T.wbuf[:, me * WW:(me + 1) * WW]
+    myx = T.xbuf[:, xcol[0]:xcol[0] + width[0]]
+
+    sy.dma_start(T.wbuf[:, me * WW:me * WW + 128], T.w1[:, :]).then_inc(T.sem.ldw, 16)
+    sc.dma_start(T.wbuf[:, me * WW + 128:(me + 1) * WW], T.w2[:, :]).then_inc(T.sem.ldw, 16)
+    sy.dma_start(myx, T.x[:, 0:width[0]]).then_inc(T.sem.ldx, 16)
+
+    helpers, direct = P["sends"][core]
+    sent = 0
+    g.wait_ge(T.sem.ldw, 32)
+    for hc in helpers:
+        sent += _put(g, T, topo, hc, myblk, myblk, T.sem["wa%d" % me], mask)
+    g.wait_ge(T.sem.ldx, 16)
+    sent += _put(g, T, topo, sib, myx, myx, T.sem.xa, mask)
+    for t in direct:
+        sent += _put(g, T, topo, t, myblk, myblk, T.sem["wa%d" % me], mask)
+    g.wait_ge(T.sem.ys, 1)
+    sent += _put(g, T, topo, sib, T.yrecv[:, 0:width[1]], T.ysend[:, 0:width[1]], T.sem.yr, mask)
+    g.wait_ge(T.sem.sent, sent)
+
+    order = P["order"][core]
+    units = []
+    for q, s in enumerate(order):
+        units += [(s, 1), (s, 0)] if q == len(order) - 1 else [(s, 0), (s, 1)]
+    nu = len(units)
+    first = dict((w, min(u for u in range(nu) if units[u][1] == w)) for w in (0, 1))
+    last = dict((w, max(u for u in range(nu) if units[u][1] == w)) for w in (0, 1))
+    yp = {0: T.yp0, 1: T.yp1}
+
+    seq = []
+    for u in range(nu):
+        seq.append((0, u))
+        if u >= LOOK:
+            seq.append((1, u - LOOK))
+    for u in range(nu - LOOK, nu):
+        seq.append((1, u))
+    seen_s, seen_x = set(), set()
+    for kind, u in seq:
+        s, w = units[u]
+        b, k = u % H, u // H
+        n = width[w]
+        if kind == 0:
+            if s not in seen_s:
+                seen_s.add(s)
+                if s == me:
+                    te.wait_ge(T.sem.ldw, 32)
+                else:
+                    te.wait_ge(T.sem["wa%d" % s], ne)
+            if w not in seen_x:
+                seen_x.add(w)
+                if w == 0:
+                    te.wait_ge(T.sem.ldx, 16)
+                else:
+                    te.wait_ge(T.sem.xa, ne)
+            if k > 0:
+                te.wait_ge(T.sem["re%d" % b], k)
+            te.matmul(T["hp%d" % b][:, 0:n], T.wbuf[:, s * WW:s * WW + 128], T.xbuf[:, xcol[w]:xcol[w] + n],
+                      True, True).then_inc(T.sem["ma%d" % b], 1)
+        else:
+            te.wait_ge(T.sem["re%d" % b], k + 1)
+            te.matmul(yp[w][:, 0:n], T.wbuf[:, s * WW + 128:(s + 1) * WW], T["hs%d" % b][:, 0:n],
+                      u == first[w], u == last[w]).then_inc(T.sem["mb%d" % b], 1)
+
+    ve.memset(T.zero[:, :], 0.0).then_inc(T.sem.zr, 1)
+    ve.wait_ge(T.sem.zr, 1)
+    for u in range(nu):
+        s, w = units[u]
+        b, k = u % H, u // H
+        n = width[w]
+        ve.wait_ge(T.sem["ma%d" % b], k + 1)
+        if k > 0:
+            ve.wait_ge(T.sem["mb%d" % b], k)
+        ve.tensor_tensor(T["hs%d" % b][:, 0:n], T["hp%d" % b][:, 0:n], T.zero[:, 0:n],
+                         AluOpType.max).then_inc(T.sem["re%d" % b], 1)
+    for u in range(max(0, nu - H), last[1] + 1):
+        ve.wait_ge(T.sem["mb%d" % (u % H)], u // H + 1)
+    ve.tensor_copy(T.ysend[:, 0:width[1]], T.yp1[:, 0:width[1]]).then_inc(T.sem.ys, 1)
+    for u in range(last[1] + 1, nu):
+        ve.wait_ge(T.sem["mb%d" % (u % H)], u // H + 1)
+    ve.wait_ge(T.sem.yr, ne)
+    ve.tensor_tensor(T.yout[:, 0:width[0]], T.yp0[:, 0:width[0]], T.yrecv[:, 0:width[0]],
+                     AluOpType.add).then_inc(T.sem.yo, 1)
+
+    sy.wait_ge(T.sem.yo, 1)
+    sy.dma_start(T.y[:, 0:width[0]], T.yout[:, 0:width[0]]).then_inc(T.sem.st, 16)
+    sy.wait_ge(T.sem.st, 16)

@@ -1,27 +1,33 @@
+from concourse.bass import DstId, RemoteDMATransfer
 from concourse.mybir import AluOpType
 
 H = 3
 LOOK = 1
 NSLOT = 8
 WW = 256
-RELAY_LAG = 5
+LAG = 4
+FWD = 2
+NPASS = 1
+NCC = 4
 
 SCRATCH = {
     "wbuf": ("sbuf", [128, NSLOT * WW], "bfloat16"),
     "xbuf": ("sbuf", [128, 1024], "bfloat16"),
     "zero": ("sbuf", [128, 512], "float32"),
-    "ysend": ("sbuf", [128, 512], "bfloat16"),
-    "yrecv": ("sbuf", [128, 512], "bfloat16"),
+    "ysend0": ("sbuf", [128, 512], "bfloat16"),
+    "ysend1": ("sbuf", [128, 512], "bfloat16"),
+    "yrecv": ("sbuf", [128, NCC * 512], "bfloat16"),
     "yout": ("sbuf", [128, 512], "bfloat16"),
     "yp0": ("psum", [128, 512], "float32"),
     "yp1": ("psum", [128, 512], "float32"),
+    "ya": ("psum", [128, 512], "float32"),
 }
 for _b in range(H):
     SCRATCH["hs%d" % _b] = ("sbuf", [128, 512], "bfloat16")
     SCRATCH["hp%d" % _b] = ("psum", [128, 512], "float32")
 
-SEMAPHORES = (["ldw", "ldx", "xa", "zr", "ys", "yr", "yo", "st", "sent"]
-              + ["wa%d" % s for s in range(NSLOT)]
+SEMAPHORES = (["ldw", "ldx", "xa0", "xa1", "zr", "ys0", "ys1", "ad", "yo", "st", "sent"]
+              + ["yr%d" % k for k in range(NCC)] + ["wa%d" % s for s in range(NSLOT)]
               + ["ma%d" % b for b in range(H)] + ["re%d" % b for b in range(H)] + ["mb%d" % b for b in range(H)])
 
 
@@ -35,34 +41,85 @@ def _plan(T, topo):
     n = len(chips)
     cidx = dict((ch, i) for i, ch in enumerate(chips))
     site = dict(((topo.chip(c), topo.die(c)), c) for c in cores)
+    dies = sorted(set(topo.die(c) for c in cores))
     everyone = range(topo.CORES_PER_CHIP * topo.CHIPS)
-    sends, relay, eta = {}, {}, {}
+
+    def ported(ch, d):
+        return [c for c in everyone if (topo.chip(c), topo.die(c)) == (ch, d) and c not in cores
+                and all(topo.may_write(c, t) for t in cores)]
+
+    comp = dict((key, [site[key], ported(key[0], key[1])[0]]) for key in site)
+    mate = dict((ch, [m for m in range(topo.CHIPS) if topo.mates(ch, m)][0]) for ch in chips)
+    eta, land, rlist, hlist = {}, {}, {}, {}
     for s in cores:
-        i, d = cidx[topo.chip(s)], topo.die(s)
-        tg = [site[(chips[(i + k) % n], d)] for k in range(1, n)]
-        direct = [t for t in tg if topo.may_write(s, t)]
-        cross = [t for t in tg if not topo.may_write(s, t)]
-        helpers = []
-        if cross:
-            helpers = [c for c in everyone
-                       if topo.chip(c) == topo.chip(s) and topo.die(c) == d and c not in cores
-                       and all(topo.may_write(c, t) for t in cross)]
-            helpers = helpers[:len(cross)]
-        for hi, hc in enumerate(helpers):
-            job = cross[hi::len(helpers)]
-            job = job[i % len(job):] + job[:i % len(job)]
-            relay[hc] = (i, job)
-            for q, t in enumerate(job):
-                eta[(t, i)] = hi + 1 + RELAY_LAG + q
-        for p, t in enumerate(direct):
-            eta[(t, i)] = len(helpers) + 2 + p
-        sends[s] = (helpers, direct)
-    order = {}
-    for t in cores:
-        me = cidx[topo.chip(t)]
-        rest = sorted((s for s in range(n) if s != me), key=lambda s: (eta[(t, s)], s))
-        order[t] = [me] + rest
-    return dict(cores=cores, chips=chips, cidx=cidx, sends=sends, relay=relay, order=order)
+        cs, d = topo.chip(s), topo.die(s)
+        i = cidx[cs]
+        lst, own = [], None
+        for k in range(1, n):
+            X = chips[(i + k) % n]
+            if topo.mates(cs, X):
+                own = X
+            elif topo.same_plane(cs, X) or mate[X] not in chips:
+                lst.append(X)
+        able = own is not None and all(topo.may_write(s, t) for t in comp[(own, d)])
+        rlist[s] = ([own] if able else []) + lst[:len(lst) - NPASS]
+        hlist[s] = ([own] if own is not None and not able else []) + lst[len(lst) - NPASS:]
+        for p, X in enumerate(rlist[s]):
+            land[(X, d, i)] = 3 + p
+        for q, X in enumerate(hlist[s]):
+            land[(X, d, i)] = 1 + LAG + q
+        for X in rlist[s] + hlist[s]:
+            near = topo.same_plane(cs, X) or topo.mates(cs, X)
+            eta[(X, d, i)] = land[(X, d, i)] + (0 if near else LAG)
+    onward = {}
+    for M in chips:
+        if mate[M] in chips:
+            for i, cs in enumerate(chips):
+                if topo.same_plane(cs, M):
+                    for d in dies:
+                        onward[(M, d, i)] = mate[M]
+                        eta[(mate[M], d, i)] = eta[(M, d, i)] + FWD
+    slots, target, fin = {}, {}, {}
+    for (ch, d), cc in comp.items():
+        me = cidx[ch]
+        order = [me] + sorted((s for s in range(n) if s != me), key=lambda s: (eta[(ch, d, s)], s))
+        for c in cc:
+            slots[c] = []
+        choice = {}
+        for s in order:
+            choice[s] = list(cc)
+            if s == me:
+                choice[s] = cc[:1]
+            elif (ch, d, s) in onward:
+                choice[s] = [c for c in cc if all(topo.may_write(c, t) for t in comp[(onward[(ch, d, s)], d)])]
+        for s in sorted(order, key=lambda s: len(choice[s]) > 1):
+            fit = [c for c in choice[s] if len(slots[c]) < n // len(cc)]
+            c = min(fit, key=lambda c: (len(slots[c]), -cc.index(c)))
+            slots[c].append(s)
+            target[(ch, d, s)] = c
+        for c in cc:
+            slots[c] = sorted(slots[c], key=order.index)
+            fin[c] = eta.get((ch, d, slots[c][-1]), 0)
+    sends, jobs = {}, {}
+    for s in cores:
+        cs, d = topo.chip(s), topo.die(s)
+        i = cidx[cs]
+
+        def first_stop(X):
+            if topo.same_plane(cs, X) or topo.mates(cs, X):
+                return target[(X, d, i)]
+            rc = ported(mate[X], d)[0]
+            jobs.setdefault(rc, []).append((land[(X, d, i)], i, target[(X, d, i)]))
+            return rc
+
+        sends[s] = [first_stop(X) for X in rlist[s]]
+        for q, X in enumerate(hlist[s]):
+            jobs.setdefault(comp[(cs, d)][1], []).append((1 + q * 0.01, i, first_stop(X)))
+    for (M, d, i), Y in onward.items():
+        jobs.setdefault(target[(M, d, i)], []).append((eta[(M, d, i)], i, target[(Y, d, i)]))
+    for c in jobs:
+        jobs[c] = sorted(jobs[c])
+    return dict(cores=cores, cidx=cidx, comp=comp, jobs=jobs, sends=sends, slots=slots, fin=fin)
 
 
 def _narrow(T, topo, core):
@@ -71,6 +128,10 @@ def _narrow(T, topo, core):
         if c != core:
             m &= topo.mask(core, c)
     return m
+
+
+def _ymask(T, topo, src, dst):
+    return topo.mask(src, dst) if T.rank_of(src) is not None else _narrow(T, topo, src)
 
 
 def _put(g, T, topo, dst, out_ap, in_ap, rsem, mask):
@@ -82,61 +143,81 @@ def _put(g, T, topo, dst, out_ap, in_ap, rsem, mask):
 
 def rank_program(g, core, T, topo):
     P = _plan(T, topo)
+    if core not in P["jobs"] and core not in P["slots"]:
+        return
     mask = _narrow(T, topo, core)
     ne = _bits(mask)
+    sent = 0
 
-    if core in P["relay"]:
-        slot, job = P["relay"][core]
-        blk = T.wbuf[:, slot * WW:(slot + 1) * WW]
-        g.wait_ge(T.sem["wa%d" % slot], ne)
-        sent = 0
-        for t in job:
-            sent += _put(g, T, topo, t, blk, blk, T.sem["wa%d" % slot], mask)
+    def pass_on():
+        tot = 0
+        for _t, slot, dst in P["jobs"].get(core, []):
+            blk = T.wbuf[:, slot * WW:(slot + 1) * WW]
+            g.wait_ge(T.sem["wa%d" % slot], ne)
+            tot += _put(g, T, topo, dst, blk, blk, T.sem["wa%d" % slot], mask)
+        return tot
+
+    if core not in P["slots"]:
+        sent += pass_on()
         g.wait_ge(T.sem.sent, sent)
         return
 
+    chip, die = topo.chip(core), topo.die(core)
+    me = P["cidx"][chip]
     rank = T.rank_of(core)
-    if rank is None:
-        return
     wid = T.tables["WID"]
-    mates = [c for c in P["cores"] if topo.chip(c) == topo.chip(core)]
-    sib = [c for c in mates if c != core][0]
-    width = {0: wid[rank], 1: wid[T.rank_of(sib)]}
-    off, o = {}, 0
-    for c in mates:
-        off[c] = o
-        o += wid[T.rank_of(c)]
-    xcol = {0: off[core], 1: off[sib]}
-    me = P["cidx"][topo.chip(core)]
-    te, ve, sy, sc = g.tensor, g.vector, g.sync, g.scalar
     myblk = T.wbuf[:, me * WW:(me + 1) * WW]
-    myx = T.xbuf[:, xcol[0]:xcol[0] + width[0]]
+    wa_me = T.sem["wa%d" % me]
+    te, ve, sy, sc = g.tensor, g.vector, g.sync, g.scalar
+    owners = [c for c in P["cores"] if topo.chip(c) == chip]
+    width = [wid[T.rank_of(c)] for c in owners]
+    xcol = [0, width[0]]
+    ccs = [c for o in owners for c in P["comp"][(chip, topo.die(o))]]
 
-    sy.dma_start(T.wbuf[:, me * WW:me * WW + 128], T.w1[:, :]).then_inc(T.sem.ldw, 16)
-    sc.dma_start(T.wbuf[:, me * WW + 128:(me + 1) * WW], T.w2[:, :]).then_inc(T.sem.ldw, 16)
-    sy.dma_start(myx, T.x[:, 0:width[0]]).then_inc(T.sem.ldx, 16)
+    if rank is not None:
+        mine = owners.index(core)
+        myx = T.xbuf[:, xcol[mine]:xcol[mine] + width[mine]]
+        sy.dma_start(T.wbuf[:, me * WW:me * WW + 128], T.w1[:, :]).then_inc(T.sem.ldw, 16)
+        sc.dma_start(T.wbuf[:, me * WW + 128:(me + 1) * WW], T.w2[:, :]).then_inc(T.sem.ldw, 16)
+        sy.dma_start(myx, T.x[:, 0:width[mine]]).then_inc(T.sem.ldx, 16)
+        g.wait_ge(T.sem.ldw, 32)
+        sent += _put(g, T, topo, P["comp"][(chip, die)][1], myblk, myblk, wa_me, mask)
+        g.wait_ge(T.sem.ldx, 16)
+        others = [c for c in ccs if c != core]
+        xmask = -1
+        for c in others:
+            xmask &= topo.mask(core, c)
+        xmask &= ~mask
+        g.remote_dma_fused([RemoteDMATransfer(
+            dst_ids=[DstId(rid=topo.addr(c)[0], pnc=topo.addr(c)[1]) for c in others], dma_engine_mask=xmask,
+            remote_sem=T.sem["xa%d" % mine], srcs=[myx], dsts=[myx for c in others])], local_sem=T.sem.sent)
+        sent += _bits(xmask)
+        nx = _bits(xmask)
+        for dst in P["sends"][core]:
+            sent += _put(g, T, topo, dst, myblk, myblk, wa_me, mask)
+    else:
+        mine = None
+        nx = _bits(topo.mask(owners[0], core) & ~_narrow(T, topo, owners[0]))
+    sent += pass_on()
 
-    helpers, direct = P["sends"][core]
-    sent = 0
-    g.wait_ge(T.sem.ldw, 32)
-    for hc in helpers:
-        sent += _put(g, T, topo, hc, myblk, myblk, T.sem["wa%d" % me], mask)
-    g.wait_ge(T.sem.ldx, 16)
-    sent += _put(g, T, topo, sib, myx, myx, T.sem.xa, mask)
-    for t in direct:
-        sent += _put(g, T, topo, t, myblk, myblk, T.sem["wa%d" % me], mask)
-    g.wait_ge(T.sem.ys, 1)
-    sent += _put(g, T, topo, sib, T.yrecv[:, 0:width[1]], T.ysend[:, 0:width[1]], T.sem.yr, mask)
-    g.wait_ge(T.sem.sent, sent)
-
-    order = P["order"][core]
+    slots = P["slots"][core]
+    away = sorted((w for w in (0, 1) if w != mine), key=lambda w: -width[w])
+    home = [w for w in (0, 1) if w == mine]
     units = []
-    for q, s in enumerate(order):
-        units += [(s, 1), (s, 0)] if q == len(order) - 1 else [(s, 0), (s, 1)]
+    for q, s in enumerate(slots):
+        units += [(s, w) for w in (away + home if q == len(slots) - 1 else home + away)]
     nu = len(units)
     first = dict((w, min(u for u in range(nu) if units[u][1] == w)) for w in (0, 1))
     last = dict((w, max(u for u in range(nu) if units[u][1] == w)) for w in (0, 1))
-    yp = {0: T.yp0, 1: T.yp1}
+    yp = [T.yp0, T.yp1]
+    ysend = [T.ysend0, T.ysend1]
+    pos = ccs.index(core)
+
+    for w in away:
+        g.wait_ge(T.sem["ys%d" % w], 1)
+        sent += _put(g, T, topo, owners[w], T.yrecv[:, pos * 512:pos * 512 + width[w]], ysend[w][:, 0:width[w]],
+                     T.sem["yr%d" % pos], _ymask(T, topo, core, owners[w]))
+    g.wait_ge(T.sem.sent, sent)
 
     seq = []
     for u in range(nu):
@@ -153,16 +234,16 @@ def rank_program(g, core, T, topo):
         if kind == 0:
             if s not in seen_s:
                 seen_s.add(s)
-                if s == me:
+                if s == me and rank is not None:
                     te.wait_ge(T.sem.ldw, 32)
                 else:
                     te.wait_ge(T.sem["wa%d" % s], ne)
             if w not in seen_x:
                 seen_x.add(w)
-                if w == 0:
+                if w == mine:
                     te.wait_ge(T.sem.ldx, 16)
                 else:
-                    te.wait_ge(T.sem.xa, ne)
+                    te.wait_ge(T.sem["xa%d" % w], nx)
             if k > 0:
                 te.wait_ge(T.sem["re%d" % b], k)
             te.matmul(T["hp%d" % b][:, 0:n], T.wbuf[:, s * WW:s * WW + 128], T.xbuf[:, xcol[w]:xcol[w] + n],
@@ -183,15 +264,32 @@ def rank_program(g, core, T, topo):
             ve.wait_ge(T.sem["mb%d" % b], k)
         ve.tensor_tensor(T["hs%d" % b][:, 0:n], T["hp%d" % b][:, 0:n], T.zero[:, 0:n],
                          AluOpType.max).then_inc(T.sem["re%d" % b], 1)
-    for u in range(max(0, nu - H), last[1] + 1):
-        ve.wait_ge(T.sem["mb%d" % (u % H)], u // H + 1)
-    ve.tensor_copy(T.ysend[:, 0:width[1]], T.yp1[:, 0:width[1]]).then_inc(T.sem.ys, 1)
-    for u in range(last[1] + 1, nu):
-        ve.wait_ge(T.sem["mb%d" % (u % H)], u // H + 1)
-    ve.wait_ge(T.sem.yr, ne)
-    ve.tensor_tensor(T.yout[:, 0:width[0]], T.yp0[:, 0:width[0]], T.yrecv[:, 0:width[0]],
-                     AluOpType.add).then_inc(T.sem.yo, 1)
+    nxt = max(0, nu - H)
+    for w in away:
+        while nxt <= last[w]:
+            ve.wait_ge(T.sem["mb%d" % (nxt % H)], nxt // H + 1)
+            nxt += 1
+        ve.tensor_copy(ysend[w][:, 0:width[w]], yp[w][:, 0:width[w]]).then_inc(T.sem["ys%d" % w], 1)
+    while nxt < nu:
+        ve.wait_ge(T.sem["mb%d" % (nxt % H)], nxt // H + 1)
+        nxt += 1
+    if rank is None:
+        return
 
+    n = width[mine]
+    givers = sorted((c for c in ccs if c != core), key=lambda c: P["fin"][c])
+    acc, spare = yp[mine], T.ya
+    for a, c in enumerate(givers):
+        k = ccs.index(c)
+        ve.wait_ge(T.sem["yr%d" % k], _bits(_ymask(T, topo, c, core)))
+        if a > 0:
+            ve.wait_ge(T.sem.ad, a)
+        part = T.yrecv[:, k * 512:k * 512 + n]
+        if a == len(givers) - 1:
+            ve.tensor_tensor(T.yout[:, 0:n], acc[:, 0:n], part, AluOpType.add).then_inc(T.sem.yo, 1)
+        else:
+            ve.tensor_tensor(spare[:, 0:n], acc[:, 0:n], part, AluOpType.add).then_inc(T.sem.ad, 1)
+            acc, spare = spare, acc
     sy.wait_ge(T.sem.yo, 1)
-    sy.dma_start(T.y[:, 0:width[0]], T.yout[:, 0:width[0]]).then_inc(T.sem.st, 16)
+    sy.dma_start(T.y[:, 0:n], T.yout[:, 0:n]).then_inc(T.sem.st, 16)
     sy.wait_ge(T.sem.st, 16)

@@ -1,38 +1,51 @@
 from concourse.bass import DstId, RemoteDMATransfer
 from concourse.mybir import AluOpType
 
-H = 3
-LOOK = 1
+H = 4
+LOOK = 2
 NSLOT = 8
 WW = 256
 LAG = 4
 FWD = 2
 NPASS = 1
 NCC = 4
+CH = 256
+NCH = 2
+XAT = (0, 2)
 
 SCRATCH = {
     "wbuf": ("sbuf", [128, NSLOT * WW], "bfloat16"),
     "xbuf": ("sbuf", [128, 1024], "bfloat16"),
     "zero": ("sbuf", [128, 512], "float32"),
-    "ysend0": ("sbuf", [128, 512], "bfloat16"),
-    "ysend1": ("sbuf", [128, 512], "bfloat16"),
+    "ysend": ("sbuf", [128, 1024], "bfloat16"),
     "yrecv": ("sbuf", [128, NCC * 512], "bfloat16"),
     "yout": ("sbuf", [128, 512], "bfloat16"),
-    "yp0": ("psum", [128, 512], "float32"),
-    "yp1": ("psum", [128, 512], "float32"),
-    "ya": ("psum", [128, 512], "float32"),
 }
+for _b in range(2 * NCH):
+    SCRATCH["yp%d" % _b] = ("psum", [128, 512], "float32")
 for _b in range(H):
     SCRATCH["hs%d" % _b] = ("sbuf", [128, 512], "bfloat16")
     SCRATCH["hp%d" % _b] = ("psum", [128, 512], "float32")
 
-SEMAPHORES = (["ldw", "ldx", "xa0", "xa1", "zr", "ys0", "ys1", "ad", "yo", "st", "sent"]
-              + ["yr%d" % k for k in range(NCC)] + ["wa%d" % s for s in range(NSLOT)]
+SEMAPHORES = (["ldw", "ldx", "zr", "sent"]
+              + ["xa%d_%d" % (w, c) for w in range(2) for c in range(NCH)] + ["ys%d" % i for i in range(2 * NCH)]
+              + ["ad%d" % c for c in range(NCH)] + ["yo%d" % c for c in range(NCH)] + ["st%d" % c for c in range(NCH)]
+              + ["yr%d_%d" % (k, c) for k in range(NCC) for c in range(NCH)] + ["wa%d" % s for s in range(NSLOT)]
               + ["ma%d" % b for b in range(H)] + ["re%d" % b for b in range(H)] + ["mb%d" % b for b in range(H)])
 
 
 def _bits(m):
     return bin(m).count("1")
+
+
+def _chunks(width):
+    out = []
+    for w, n in enumerate(width):
+        k = -(-n // CH)
+        step = -(-n // (k * 8)) * 8
+        for c in range(k):
+            out.append((w, c, c * step, min(step, n - c * step)))
+    return out
 
 
 def _plan(T, topo):
@@ -172,6 +185,8 @@ def rank_program(g, core, T, topo):
     owners = [c for c in P["cores"] if topo.chip(c) == chip]
     width = [wid[T.rank_of(c)] for c in owners]
     xcol = [0, width[0]]
+    cks = _chunks(width)
+    col = [xcol[w] + off for (w, _c, off, _n) in cks]
     ccs = [c for o in owners for c in P["comp"][(chip, topo.die(o))]]
 
     if rank is not None:
@@ -182,41 +197,55 @@ def rank_program(g, core, T, topo):
         sy.dma_start(myx, T.x[:, 0:width[mine]]).then_inc(T.sem.ldx, 16)
         g.wait_ge(T.sem.ldw, 32)
         sent += _put(g, T, topo, P["comp"][(chip, die)][1], myblk, myblk, wa_me, mask)
-        g.wait_ge(T.sem.ldx, 16)
         others = [c for c in ccs if c != core]
         xmask = -1
         for c in others:
             xmask &= topo.mask(core, c)
         xmask &= ~mask
-        g.remote_dma_fused([RemoteDMATransfer(
-            dst_ids=[DstId(rid=topo.addr(c)[0], pnc=topo.addr(c)[1]) for c in others], dma_engine_mask=xmask,
-            remote_sem=T.sem["xa%d" % mine], srcs=[myx], dsts=[myx for c in others])], local_sem=T.sem.sent)
-        sent += _bits(xmask)
         nx = _bits(xmask)
-        for dst in P["sends"][core]:
-            sent += _put(g, T, topo, dst, myblk, myblk, wa_me, mask)
+
+        def send_x(i):
+            ap = T.xbuf[:, col[i]:col[i] + cks[i][3]]
+            g.remote_dma_fused([RemoteDMATransfer(
+                dst_ids=[DstId(rid=topo.addr(c)[0], pnc=topo.addr(c)[1]) for c in others], dma_engine_mask=xmask,
+                remote_sem=T.sem["xa%d_%d" % (mine, cks[i][1])], srcs=[ap], dsts=[ap for c in others])],
+                local_sem=T.sem.sent)
+            return nx
+
+        xs = [i for i in range(len(cks)) if cks[i][0] == mine]
+        todo = list(P["sends"][core])
+        for q in range(len(todo) + 1):
+            for i in xs:
+                if min(XAT[cks[i][1]], len(todo)) == q:
+                    if i == xs[0]:
+                        g.wait_ge(T.sem.ldx, 16)
+                    sent += send_x(i)
+            if q < len(todo):
+                sent += _put(g, T, topo, todo[q], myblk, myblk, wa_me, mask)
     else:
         mine = None
         nx = _bits(topo.mask(owners[0], core) & ~_narrow(T, topo, owners[0]))
     sent += pass_on()
 
     slots = P["slots"][core]
-    away = sorted((w for w in (0, 1) if w != mine), key=lambda w: -width[w])
-    home = [w for w in (0, 1) if w == mine]
+    home = [i for i in range(len(cks)) if cks[i][0] == mine]
+    away = [i for i in range(len(cks)) if cks[i][0] != mine]
+    early = sorted(away, key=lambda i: (cks[i][1], cks[i][3], i))
+    final = sorted(away, key=lambda i: (-width[cks[i][0]], i))
     units = []
     for q, s in enumerate(slots):
-        units += [(s, w) for w in (away + home if q == len(slots) - 1 else home + away)]
+        units += [(s, i) for i in (final + home if q == len(slots) - 1 else home + early)]
     nu = len(units)
-    first = dict((w, min(u for u in range(nu) if units[u][1] == w)) for w in (0, 1))
-    last = dict((w, max(u for u in range(nu) if units[u][1] == w)) for w in (0, 1))
-    yp = [T.yp0, T.yp1]
-    ysend = [T.ysend0, T.ysend1]
+    first = dict((i, min(u for u in range(nu) if units[u][1] == i)) for i in range(len(cks)))
+    last = dict((i, max(u for u in range(nu) if units[u][1] == i)) for i in range(len(cks)))
+    yp = [T["yp%d" % i] for i in range(len(cks))]
     pos = ccs.index(core)
 
-    for w in away:
-        g.wait_ge(T.sem["ys%d" % w], 1)
-        sent += _put(g, T, topo, owners[w], T.yrecv[:, pos * 512:pos * 512 + width[w]], ysend[w][:, 0:width[w]],
-                     T.sem["yr%d" % pos], _ymask(T, topo, core, owners[w]))
+    for i in final:
+        w, c, off, n = cks[i]
+        g.wait_ge(T.sem["ys%d" % i], 1)
+        sent += _put(g, T, topo, owners[w], T.yrecv[:, pos * 512 + off:pos * 512 + off + n],
+                     T.ysend[:, col[i]:col[i] + n], T.sem["yr%d_%d" % (pos, c)], _ymask(T, topo, core, owners[w]))
     g.wait_ge(T.sem.sent, sent)
 
     seq = []
@@ -228,9 +257,9 @@ def rank_program(g, core, T, topo):
         seq.append((1, u))
     seen_s, seen_x = set(), set()
     for kind, u in seq:
-        s, w = units[u]
+        s, i = units[u]
         b, k = u % H, u // H
-        n = width[w]
+        w, c, _off, n = cks[i]
         if kind == 0:
             if s not in seen_s:
                 seen_s.add(s)
@@ -238,58 +267,66 @@ def rank_program(g, core, T, topo):
                     te.wait_ge(T.sem.ldw, 32)
                 else:
                     te.wait_ge(T.sem["wa%d" % s], ne)
-            if w not in seen_x:
-                seen_x.add(w)
+            if i not in seen_x:
+                seen_x.add(i)
                 if w == mine:
                     te.wait_ge(T.sem.ldx, 16)
                 else:
-                    te.wait_ge(T.sem["xa%d" % w], nx)
+                    te.wait_ge(T.sem["xa%d_%d" % (w, c)], nx)
             if k > 0:
                 te.wait_ge(T.sem["re%d" % b], k)
-            te.matmul(T["hp%d" % b][:, 0:n], T.wbuf[:, s * WW:s * WW + 128], T.xbuf[:, xcol[w]:xcol[w] + n],
+            te.matmul(T["hp%d" % b][:, 0:n], T.wbuf[:, s * WW:s * WW + 128], T.xbuf[:, col[i]:col[i] + n],
                       True, True).then_inc(T.sem["ma%d" % b], 1)
         else:
             te.wait_ge(T.sem["re%d" % b], k + 1)
-            te.matmul(yp[w][:, 0:n], T.wbuf[:, s * WW + 128:(s + 1) * WW], T["hs%d" % b][:, 0:n],
-                      u == first[w], u == last[w]).then_inc(T.sem["mb%d" % b], 1)
+            te.matmul(yp[i][:, 0:n], T.wbuf[:, s * WW + 128:(s + 1) * WW], T["hs%d" % b][:, 0:n],
+                      u == first[i], u == last[i]).then_inc(T.sem["mb%d" % b], 1)
+
+    got = [0] * H
+
+    def done(us):
+        for b in range(H):
+            k = max([u // H + 1 for u in us if u % H == b] + [0])
+            if k > got[b]:
+                ve.wait_ge(T.sem["mb%d" % b], k)
+                got[b] = k
 
     ve.memset(T.zero[:, :], 0.0).then_inc(T.sem.zr, 1)
     ve.wait_ge(T.sem.zr, 1)
-    for u in range(nu):
-        s, w = units[u]
+    for kind, u in seq:
+        s, i = units[u]
         b, k = u % H, u // H
-        n = width[w]
-        ve.wait_ge(T.sem["ma%d" % b], k + 1)
-        if k > 0:
-            ve.wait_ge(T.sem["mb%d" % b], k)
-        ve.tensor_tensor(T["hs%d" % b][:, 0:n], T["hp%d" % b][:, 0:n], T.zero[:, 0:n],
-                         AluOpType.max).then_inc(T.sem["re%d" % b], 1)
-    nxt = max(0, nu - H)
-    for w in away:
-        while nxt <= last[w]:
-            ve.wait_ge(T.sem["mb%d" % (nxt % H)], nxt // H + 1)
-            nxt += 1
-        ve.tensor_copy(ysend[w][:, 0:width[w]], yp[w][:, 0:width[w]]).then_inc(T.sem["ys%d" % w], 1)
-    while nxt < nu:
-        ve.wait_ge(T.sem["mb%d" % (nxt % H)], nxt // H + 1)
-        nxt += 1
+        n = cks[i][3]
+        if kind == 0:
+            ve.wait_ge(T.sem["ma%d" % b], k + 1)
+            if k > 0:
+                done([u - H])
+            ve.tensor_tensor(T["hs%d" % b][:, 0:n], T["hp%d" % b][:, 0:n], T.zero[:, 0:n],
+                             AluOpType.max).then_inc(T.sem["re%d" % b], 1)
+        elif u == last[i] and i in away:
+            done([v for v in range(nu) if units[v][1] == i])
+            ve.tensor_copy(T.ysend[:, col[i]:col[i] + n], yp[i][:, 0:n]).then_inc(T.sem["ys%d" % i], 1)
+    done(range(nu))
     if rank is None:
         return
 
-    n = width[mine]
     givers = sorted((c for c in ccs if c != core), key=lambda c: P["fin"][c])
-    acc, spare = yp[mine], T.ya
-    for a, c in enumerate(givers):
-        k = ccs.index(c)
-        ve.wait_ge(T.sem["yr%d" % k], _bits(_ymask(T, topo, c, core)))
-        if a > 0:
-            ve.wait_ge(T.sem.ad, a)
-        part = T.yrecv[:, k * 512:k * 512 + n]
-        if a == len(givers) - 1:
-            ve.tensor_tensor(T.yout[:, 0:n], acc[:, 0:n], part, AluOpType.add).then_inc(T.sem.yo, 1)
-        else:
-            ve.tensor_tensor(spare[:, 0:n], acc[:, 0:n], part, AluOpType.add).then_inc(T.sem.ad, 1)
-            acc, spare = spare, acc
-    sy.wait_ge(T.sem.yo, 1)
-    sy.dma_start(T.y[:, 0:n], T.yout[:, 0:n]).then_inc(T.sem.st, 16)
-    sy.wait_ge(T.sem.st, 16)
+    for a, gv in enumerate(givers):
+        k = ccs.index(gv)
+        for i in home:
+            _w, c, off, n = cks[i]
+            ve.wait_ge(T.sem["yr%d_%d" % (k, c)], _bits(_ymask(T, topo, gv, core)))
+            if a > 0:
+                ve.wait_ge(T.sem["ad%d" % c], a)
+            part = T.yrecv[:, k * 512 + off:k * 512 + off + n]
+            if a == len(givers) - 1:
+                ve.tensor_tensor(T.yout[:, off:off + n], yp[i][:, 0:n], part, AluOpType.add).then_inc(
+                    T.sem["yo%d" % c], 1)
+            else:
+                ve.tensor_tensor(yp[i][:, 0:n], yp[i][:, 0:n], part, AluOpType.add).then_inc(T.sem["ad%d" % c], 1)
+    for i in home:
+        _w, c, off, n = cks[i]
+        q = (sy, sc)[c % 2]
+        q.wait_ge(T.sem["yo%d" % c], 1)
+        q.dma_start(T.y[:, off:off + n], T.yout[:, off:off + n]).then_inc(T.sem["st%d" % c], 16)
+        q.wait_ge(T.sem["st%d" % c], 16)

from concourse.bass import DstId, RemoteDMATransfer
from concourse.mybir import AluOpType

H = 4
LOOK = 2
NSLOT = 8
WW = 256
LAG = 4
FWD = 2
NPASS = 1
NCC = 4
CH = 256
NCH = 2
XAT = (0, 2)

SCRATCH = {
    "wbuf": ("sbuf", [128, NSLOT * WW], "bfloat16"),
    "xbuf": ("sbuf", [128, 1024], "bfloat16"),
    "zero": ("sbuf", [128, 512], "float32"),
    "ysend": ("sbuf", [128, 1024], "bfloat16"),
    "yrecv": ("sbuf", [128, NCC * 512], "bfloat16"),
    "yout": ("sbuf", [128, 512], "bfloat16"),
}
for _b in range(2 * NCH):
    SCRATCH["yp%d" % _b] = ("psum", [128, 512], "float32")
for _b in range(H):
    SCRATCH["hs%d" % _b] = ("sbuf", [128, 512], "bfloat16")
    SCRATCH["hp%d" % _b] = ("psum", [128, 512], "float32")

SEMAPHORES = (["ldw", "ldx", "zr", "sent"]
              + ["xa%d_%d" % (w, c) for w in range(2) for c in range(NCH)] + ["ys%d" % i for i in range(2 * NCH)]
              + ["ad%d" % c for c in range(NCH)] + ["yo%d" % c for c in range(NCH)] + ["st%d" % c for c in range(NCH)]
              + ["yr%d_%d" % (k, c) for k in range(NCC) for c in range(NCH)] + ["wa%d" % s for s in range(NSLOT)]
              + ["ma%d" % b for b in range(H)] + ["re%d" % b for b in range(H)] + ["mb%d" % b for b in range(H)])


def _bits(m):
    return bin(m).count("1")


def _chunks(width):
    out = []
    for w, n in enumerate(width):
        k = -(-n // CH)
        step = -(-n // (k * 8)) * 8
        for c in range(k):
            out.append((w, c, c * step, min(step, n - c * step)))
    return out


def _plan(T, topo):
    cores = list(T.cores)
    chips = sorted(set(topo.chip(c) for c in cores))
    n = len(chips)
    cidx = dict((ch, i) for i, ch in enumerate(chips))
    site = dict(((topo.chip(c), topo.die(c)), c) for c in cores)
    dies = sorted(set(topo.die(c) for c in cores))
    everyone = range(topo.CORES_PER_CHIP * topo.CHIPS)

    def ported(ch, d):
        return [c for c in everyone if (topo.chip(c), topo.die(c)) == (ch, d) and c not in cores
                and all(topo.may_write(c, t) for t in cores)]

    comp = dict((key, [site[key], ported(key[0], key[1])[0]]) for key in site)
    mate = dict((ch, [m for m in range(topo.CHIPS) if topo.mates(ch, m)][0]) for ch in chips)
    eta, land, rlist, hlist = {}, {}, {}, {}
    for s in cores:
        cs, d = topo.chip(s), topo.die(s)
        i = cidx[cs]
        lst, own = [], None
        for k in range(1, n):
            X = chips[(i + k) % n]
            if topo.mates(cs, X):
                own = X
            elif topo.same_plane(cs, X) or mate[X] not in chips:
                lst.append(X)
        able = own is not None and all(topo.may_write(s, t) for t in comp[(own, d)])
        rlist[s] = ([own] if able else []) + lst[:len(lst) - NPASS]
        hlist[s] = ([own] if own is not None and not able else []) + lst[len(lst) - NPASS:]
        for p, X in enumerate(rlist[s]):
            land[(X, d, i)] = 3 + p
        for q, X in enumerate(hlist[s]):
            land[(X, d, i)] = 1 + LAG + q
        for X in rlist[s] + hlist[s]:
            near = topo.same_plane(cs, X) or topo.mates(cs, X)
            eta[(X, d, i)] = land[(X, d, i)] + (0 if near else LAG)
    onward = {}
    for M in chips:
        if mate[M] in chips:
            for i, cs in enumerate(chips):
                if topo.same_plane(cs, M):
                    for d in dies:
                        onward[(M, d, i)] = mate[M]
                        eta[(mate[M], d, i)] = eta[(M, d, i)] + FWD
    slots, target, fin = {}, {}, {}
    for (ch, d), cc in comp.items():
        me = cidx[ch]
        order = [me] + sorted((s for s in range(n) if s != me), key=lambda s: (eta[(ch, d, s)], s))
        for c in cc:
            slots[c] = []
        choice = {}
        for s in order:
            choice[s] = list(cc)
            if s == me:
                choice[s] = cc[:1]
            elif (ch, d, s) in onward:
                choice[s] = [c for c in cc if all(topo.may_write(c, t) for t in comp[(onward[(ch, d, s)], d)])]
        for s in sorted(order, key=lambda s: len(choice[s]) > 1):
            fit = [c for c in choice[s] if len(slots[c]) < n // len(cc)]
            c = min(fit, key=lambda c: (len(slots[c]), -cc.index(c)))
            slots[c].append(s)
            target[(ch, d, s)] = c
        for c in cc:
            slots[c] = sorted(slots[c], key=order.index)
            fin[c] = eta.get((ch, d, slots[c][-1]), 0)
    sends, jobs = {}, {}
    for s in cores:
        cs, d = topo.chip(s), topo.die(s)
        i = cidx[cs]

        def first_stop(X):
            if topo.same_plane(cs, X) or topo.mates(cs, X):
                return target[(X, d, i)]
            rc = ported(mate[X], d)[0]
            jobs.setdefault(rc, []).append((land[(X, d, i)], i, target[(X, d, i)]))
            return rc

        sends[s] = [first_stop(X) for X in rlist[s]]
        for q, X in enumerate(hlist[s]):
            jobs.setdefault(comp[(cs, d)][1], []).append((1 + q * 0.01, i, first_stop(X)))
    for (M, d, i), Y in onward.items():
        jobs.setdefault(target[(M, d, i)], []).append((eta[(M, d, i)], i, target[(Y, d, i)]))
    for c in jobs:
        jobs[c] = sorted(jobs[c])
    return dict(cores=cores, cidx=cidx, comp=comp, jobs=jobs, sends=sends, slots=slots, fin=fin)


def _narrow(T, topo, core):
    m = -1
    for c in T.cores:
        if c != core:
            m &= topo.mask(core, c)
    return m


def _ymask(T, topo, src, dst):
    return topo.mask(src, dst) if T.rank_of(src) is not None else _narrow(T, topo, src)


def _put(g, T, topo, dst, out_ap, in_ap, rsem, mask):
    rid, pid, _se = topo.addr(dst)
    g.remote_dma(out_ap=out_ap, in_ap=in_ap, remote_sem=rsem, local_sem=T.sem.sent, pid=pid, routing_id=rid,
                 dma_engine_mask=mask)
    return _bits(mask)


def rank_program(g, core, T, topo):
    P = _plan(T, topo)
    if core not in P["jobs"] and core not in P["slots"]:
        return
    mask = _narrow(T, topo, core)
    ne = _bits(mask)
    sent = 0

    def pass_on():
        tot = 0
        for _t, slot, dst in P["jobs"].get(core, []):
            blk = T.wbuf[:, slot * WW:(slot + 1) * WW]
            g.wait_ge(T.sem["wa%d" % slot], ne)
            tot += _put(g, T, topo, dst, blk, blk, T.sem["wa%d" % slot], mask)
        return tot

    if core not in P["slots"]:
        sent += pass_on()
        g.wait_ge(T.sem.sent, sent)
        return

    chip, die = topo.chip(core), topo.die(core)
    me = P["cidx"][chip]
    rank = T.rank_of(core)
    wid = T.tables["WID"]
    myblk = T.wbuf[:, me * WW:(me + 1) * WW]
    wa_me = T.sem["wa%d" % me]
    te, ve, sy, sc = g.tensor, g.vector, g.sync, g.scalar
    owners = [c for c in P["cores"] if topo.chip(c) == chip]
    width = [wid[T.rank_of(c)] for c in owners]
    xcol = [0, width[0]]
    cks = _chunks(width)
    col = [xcol[w] + off for (w, _c, off, _n) in cks]
    ccs = [c for o in owners for c in P["comp"][(chip, topo.die(o))]]

    if rank is not None:
        mine = owners.index(core)
        myx = T.xbuf[:, xcol[mine]:xcol[mine] + width[mine]]
        sy.dma_start(T.wbuf[:, me * WW:me * WW + 128], T.w1[:, :]).then_inc(T.sem.ldw, 16)
        sc.dma_start(T.wbuf[:, me * WW + 128:(me + 1) * WW], T.w2[:, :]).then_inc(T.sem.ldw, 16)
        sy.dma_start(myx, T.x[:, 0:width[mine]]).then_inc(T.sem.ldx, 16)
        g.wait_ge(T.sem.ldw, 32)
        sent += _put(g, T, topo, P["comp"][(chip, die)][1], myblk, myblk, wa_me, mask)
        others = [c for c in ccs if c != core]
        xmask = -1
        for c in others:
            xmask &= topo.mask(core, c)
        xmask &= ~mask
        nx = _bits(xmask)

        def send_x(i):
            ap = T.xbuf[:, col[i]:col[i] + cks[i][3]]
            g.remote_dma_fused([RemoteDMATransfer(
                dst_ids=[DstId(rid=topo.addr(c)[0], pnc=topo.addr(c)[1]) for c in others], dma_engine_mask=xmask,
                remote_sem=T.sem["xa%d_%d" % (mine, cks[i][1])], srcs=[ap], dsts=[ap for c in others])],
                local_sem=T.sem.sent)
            return nx

        xs = [i for i in range(len(cks)) if cks[i][0] == mine]
        todo = list(P["sends"][core])
        for q in range(len(todo) + 1):
            for i in xs:
                if min(XAT[cks[i][1]], len(todo)) == q:
                    if i == xs[0]:
                        g.wait_ge(T.sem.ldx, 16)
                    sent += send_x(i)
            if q < len(todo):
                sent += _put(g, T, topo, todo[q], myblk, myblk, wa_me, mask)
    else:
        mine = None
        nx = _bits(topo.mask(owners[0], core) & ~_narrow(T, topo, owners[0]))
    sent += pass_on()

    slots = P["slots"][core]
    home = [i for i in range(len(cks)) if cks[i][0] == mine]
    away = [i for i in range(len(cks)) if cks[i][0] != mine]
    early = sorted(away, key=lambda i: (cks[i][1], cks[i][3], i))
    final = sorted(away, key=lambda i: (-width[cks[i][0]], i))
    units = []
    for q, s in enumerate(slots):
        units += [(s, i) for i in (final + home if q == len(slots) - 1 else home + early)]
    nu = len(units)
    first = dict((i, min(u for u in range(nu) if units[u][1] == i)) for i in range(len(cks)))
    last = dict((i, max(u for u in range(nu) if units[u][1] == i)) for i in range(len(cks)))
    yp = [T["yp%d" % i] for i in range(len(cks))]
    pos = ccs.index(core)

    for i in final:
        w, c, off, n = cks[i]
        g.wait_ge(T.sem["ys%d" % i], 1)
        sent += _put(g, T, topo, owners[w], T.yrecv[:, pos * 512 + off:pos * 512 + off + n],
                     T.ysend[:, col[i]:col[i] + n], T.sem["yr%d_%d" % (pos, c)], _ymask(T, topo, core, owners[w]))
    g.wait_ge(T.sem.sent, sent)

    seq = []
    for u in range(nu):
        seq.append((0, u))
        if u >= LOOK:
            seq.append((1, u - LOOK))
    for u in range(nu - LOOK, nu):
        seq.append((1, u))
    seen_s, seen_x = set(), set()
    for kind, u in seq:
        s, i = units[u]
        b, k = u % H, u // H
        w, c, _off, n = cks[i]
        if kind == 0:
            if s not in seen_s:
                seen_s.add(s)
                if s == me and rank is not None:
                    te.wait_ge(T.sem.ldw, 32)
                else:
                    te.wait_ge(T.sem["wa%d" % s], ne)
            if i not in seen_x:
                seen_x.add(i)
                if w == mine:
                    te.wait_ge(T.sem.ldx, 16)
                else:
                    te.wait_ge(T.sem["xa%d_%d" % (w, c)], nx)
            if k > 0:
                te.wait_ge(T.sem["re%d" % b], k)
            te.matmul(T["hp%d" % b][:, 0:n], T.wbuf[:, s * WW:s * WW + 128], T.xbuf[:, col[i]:col[i] + n],
                      True, True).then_inc(T.sem["ma%d" % b], 1)
        else:
            te.wait_ge(T.sem["re%d" % b], k + 1)
            te.matmul(yp[i][:, 0:n], T.wbuf[:, s * WW + 128:(s + 1) * WW], T["hs%d" % b][:, 0:n],
                      u == first[i], u == last[i]).then_inc(T.sem["mb%d" % b], 1)

    got = [0] * H

    def done(us):
        for b in range(H):
            k = max([u // H + 1 for u in us if u % H == b] + [0])
            if k > got[b]:
                ve.wait_ge(T.sem["mb%d" % b], k)
                got[b] = k

    ve.memset(T.zero[:, :], 0.0).then_inc(T.sem.zr, 1)
    ve.wait_ge(T.sem.zr, 1)
    for kind, u in seq:
        s, i = units[u]
        b, k = u % H, u // H
        n = cks[i][3]
        if kind == 0:
            ve.wait_ge(T.sem["ma%d" % b], k + 1)
            if k > 0:
                done([u - H])
            ve.tensor_tensor(T["hs%d" % b][:, 0:n], T["hp%d" % b][:, 0:n], T.zero[:, 0:n],
                             AluOpType.max).then_inc(T.sem["re%d" % b], 1)
        elif u == last[i] and i in away:
            done([v for v in range(nu) if units[v][1] == i])
            ve.tensor_copy(T.ysend[:, col[i]:col[i] + n], yp[i][:, 0:n]).then_inc(T.sem["ys%d" % i], 1)
    done(range(nu))
    if rank is None:
        return

    givers = sorted((c for c in ccs if c != core), key=lambda c: P["fin"][c])
    for a, gv in enumerate(givers):
        k = ccs.index(gv)
        for i in home:
            _w, c, off, n = cks[i]
            ve.wait_ge(T.sem["yr%d_%d" % (k, c)], _bits(_ymask(T, topo, gv, core)))
            if a > 0:
                ve.wait_ge(T.sem["ad%d" % c], a)
            part = T.yrecv[:, k * 512 + off:k * 512 + off + n]
            if a == len(givers) - 1:
                ve.tensor_tensor(T.yout[:, off:off + n], yp[i][:, 0:n], part, AluOpType.add).then_inc(
                    T.sem["yo%d" % c], 1)
            else:
                ve.tensor_tensor(yp[i][:, 0:n], yp[i][:, 0:n], part, AluOpType.add).then_inc(T.sem["ad%d" % c], 1)
    for i in home:
        _w, c, off, n = cks[i]
        q = (sy, sc)[c % 2]
        q.wait_ge(T.sem["yo%d" % c], 1)
        q.dma_start(T.y[:, off:off + n], T.yout[:, off:off + n]).then_inc(T.sem["st%d" % c], 16)
        q.wait_ge(T.sem["st%d" % c], 16)
